import numpy as np
import ml_dtypes


def mxq(x, axis, fmt="e4m3"):
    dtype, down = {"e4m3": (ml_dtypes.float8_e4m3fn, 7), "e5m2": (ml_dtypes.float8_e5m2, 14)}[fmt]
    v = np.moveaxis(np.asarray(x, np.float32).astype(ml_dtypes.bfloat16).astype(np.float64), axis, -1)
    blocks = v.reshape(v.shape[:-1] + (-1, 32))
    amax = np.abs(blocks).max(-1, keepdims=True)
    byte = np.maximum(np.where(amax > 0, np.frexp(amax)[1] - 1 + 127, 0) - down, 1)
    scale = np.exp2(byte - 127.0)
    codes = (blocks / scale).astype(np.float32).astype(dtype).astype(np.float64)
    return np.moveaxis((codes * scale).reshape(v.shape), -1, axis)


WIDE = False


def mx_kscale(k):
    if not WIDE:
        return np.ones(k)
    levels = np.array([10, -10, 5, -5, 0])
    if k % 512:
        return np.exp2(np.random.permutation(np.resize(levels, k // 32))).repeat(32)
    a = np.empty((k // 512, 16))
    for p in range(k // 512):
        a[p, :8] = np.random.permutation(np.resize(levels, 8))
        for g in range(8):
            far = levels[np.abs(levels - a[p, g]) >= 10]
            a[p, g + 8] = far[np.random.randint(len(far))]
    return np.exp2(a.ravel()).repeat(32)


def f64(x):
    return np.asarray(x).astype(np.float64)


def striped(idx):
    return np.tile(idx.reshape(-1, 16).T, (8, 1)).astype(np.uint16)


def unstriped(offs):
    return offs[:16].T.reshape(-1).astype(np.int64)


def striped8(idx):
    return np.concatenate([x.reshape(-1, 16).T for x in idx]).astype(np.uint16)


def runs(offs, k):
    lists = np.stack([offs[16 * r : 16 * r + 16].T.reshape(-1) for r in range(8)]).astype(np.int64)
    return lists[np.arange(k) % 512 // 64]


def pack_weight(w):
    k, n = w.shape
    w = f64(np.asarray(w, np.float32).astype(ml_dtypes.bfloat16)).reshape(k // 32, 32, n)
    amax = np.abs(w).max(1)
    byte = np.clip(np.where(amax > 0, np.frexp(amax)[1] - 1 + 127 - 7, 1), 1, 254)
    scaled = (w * np.exp2(127.0 - byte)[:, None, :]).reshape(k, n).astype(np.float32)
    words = np.ascontiguousarray(scaled.reshape(k // 512, 128, 4, n).transpose(0, 1, 3, 2)).astype(ml_dtypes.float8_e4m3fn).view(np.uint8)
    return words, np.ascontiguousarray(byte.astype(np.uint8).reshape(k // 512, 16, n))


def unpack_weight(words, scales):
    g, p, n, _ = words.shape
    vals = np.ascontiguousarray(words).view(ml_dtypes.float8_e4m3fn).astype(np.float64) * np.repeat(np.exp2(scales.astype(np.float64) - 127.0), 8, axis=1)[..., None]
    return vals.transpose(0, 1, 3, 2).reshape(g * 512, n)


K, T, S, G, H, W = 512, 1024, 256, 2048, 512, 128


def setup_inputs():
    n = np.random.standard_normal
    s = mx_kscale(K)[:, None]
    packed_xT = pack_weight(n((K, T)) * s)
    packed_dT = pack_weight(n((K, G)) / s)
    perm = np.random.permutation(S)
    perm2 = np.random.permutation(S)
    perm3 = np.random.permutation(S)
    return {
        "x_words": packed_xT[0],
        "x_scales": packed_xT[1],
        "d_words": packed_dT[0],
        "d_scales": packed_dT[1],
        "gs": (np.random.uniform(0.5, 1.5, (K, 1)) * s).astype(np.float32),
        "offs": striped(np.random.permutation(T)[:S]),
        "k1": striped8(np.random.randint(0, G, (8, H))),
        "two": striped(np.random.permutation(T)[:S]),
        "k2": striped8(np.random.randint(0, G, (8, H))),
        "n1": striped(perm[:W]),
        "n2": striped(perm[W:]),
        "k3": striped8(np.random.randint(0, G, (8, H))),
        "k4": striped8(np.random.randint(0, G, (8, H))),
        "duo": striped(np.random.permutation(T)[:S]),
        "k5": striped8(np.random.randint(0, G, (8, H))),
        "hz": striped8(np.random.randint(0, T, (8, S))),
        "n3": striped(perm2[:W]),
        "n4": striped(perm2[W:]),
        "n5": striped(perm3[:W]),
        "n6": striped(perm3[W:]),
    }


def reference(x_words, x_scales, d_words, d_scales, gs, offs, k1, two, k2, n1, n2, k3, k4, duo, k5, hz, n3, n4, n5, n6):
    d_k3 = unpack_weight(d_words, d_scales)[np.arange(K)[:, None], runs(k3, K)]
    d_k1 = unpack_weight(d_words, d_scales)[np.arange(K)[:, None], runs(k1, K)]
    xq = unpack_weight(x_words, x_scales)[:, unstriped(offs)]
    d_k2 = unpack_weight(d_words, d_scales)[np.arange(K)[:, None], runs(k2, K)]
    x_two = unpack_weight(x_words, x_scales)[:, unstriped(two)]
    h = 0.0625 * (d_k1.T @ xq + d_k2.T @ x_two)
    pa = h[:, unstriped(n1)]
    pb = h[:, unstriped(n2)]
    rb = np.maximum(pa, pb)
    ra = pa / (np.abs(pb) + 0.5)
    ua = np.zeros((H, S))
    ua[:, unstriped(n1)] = ra
    ub = ua.copy()
    ub[:, unstriped(n2)] = rb
    z = f64(gs) * ub
    d_k4 = unpack_weight(d_words, d_scales)[np.arange(K)[:, None], runs(k4, K)]
    x_duo = unpack_weight(x_words, x_scales)[:, unstriped(duo)]
    d_k5 = unpack_weight(d_words, d_scales)[np.arange(K)[:, None], runs(k5, K)]
    x_hz = unpack_weight(x_words, x_scales)[np.arange(K)[:, None], runs(hz, K)]
    h2 = 0.0625 * ((d_k3.T @ mxq(z, 0, "e4m3") + d_k4.T @ x_duo + d_k5.T @ x_hz))
    pa2 = h2[:, unstriped(n3)]
    pb2 = h2[:, unstriped(n4)]
    rb2 = np.minimum(pa2, pb2)
    ra2 = np.maximum(pa2, pb2)
    ua2 = np.zeros((H, S))
    ua2[:, unstriped(n5)] = ra2
    ub2 = ua2.copy()
    ub2[:, unstriped(n6)] = rb2
    return ub2 - h2

@@ -1,0 +1,253 @@
+from contextlib import ExitStack
+
+import concourse.mybir as mybir
+
+K, T, S, G, H, W = 512, 1024, 256, 2048, 512, 128
+FLOPS = 5 * 2 * K * H * S
+
+F32 = mybir.dt.float32
+BF16 = mybir.dt.bfloat16
+I32 = mybir.dt.int32
+U32 = mybir.dt.uint32
+U16 = mybir.dt.uint16
+U8 = mybir.dt.uint8
+FP8X4 = mybir.dt.float8_e4m3fn_x4
+ALU = mybir.AluOpType
+ACT = mybir.ActivationFunctionType
+P = 128
+HALF = H // 2
+
+
+def tile_picked_mttzmthratiocpor_none_p_kernel(
+    tc, x_words, x_scales, d_words, d_scales, gs, offs, k1, two, k2, n1, n2, k3, k4, duo, k5, hz, n3, n4, n5, n6, out
+):
+    nc = tc.nc
+    with ExitStack() as ctx:
+        lists = ctx.enter_context(tc.tile_pool(name="lists", bufs=1))
+        sb = ctx.enter_context(tc.tile_pool(name="sb", bufs=1))
+        psum = ctx.enter_context(tc.psum_pool(name="psum", bufs=1))
+
+        def tile(shape, dtype, name, tag=None):
+            return sb.tile(shape, dtype, name=name, tag=tag or name, align_bytes=64)
+
+        def load_list(src, name):
+            t = lists.tile(list(src.shape), U16, name=name)
+            nc.sync.dma_start(t[:], src)
+            return t
+
+        ds = tile([P, G], U8, "ds")
+        nc.sync.dma_start(ds[:].bitcast(I32), d_scales[0].bitcast(I32).unsqueeze(1).to_broadcast([16, 8, G // 4]))
+        l_k1 = load_list(k1, "l_k1")
+        l_k2 = load_list(k2, "l_k2")
+        xs = tile([P, T], U8, "xs")
+        for q in range(4):
+            nc.sync.dma_start(
+                xs[32 * q : 32 * (q + 1), :].bitcast(I32),
+                x_scales[0][4 * q : 4 * (q + 1), :].bitcast(I32).unsqueeze(0).to_broadcast([8, 4, T // 4]),
+            )
+        xw = tile([P, T], U32, "xw")
+        nc.sync.dma_start(xw[:].bitcast(I32), x_words[0].rearrange("p n t -> p (n t)").bitcast(I32))
+        l_offs = load_list(offs, "l_offs")
+        l_two = load_list(two, "l_two")
+        dw = tile([P, G], U32, "dw")
+        nc.sync.dma_start(dw[:].bitcast(I32), d_words[0].rearrange("p n t -> p (n t)").bitcast(I32))
+        l_n2 = load_list(n2, "l_n2")
+        l_n1 = load_list(n1, "l_n1")
+        l_hz = load_list(hz, "l_hz")
+        l_duo = load_list(duo, "l_duo")
+        l_k4 = load_list(k4, "l_k4")
+        l_k5 = load_list(k5, "l_k5")
+        l_k3 = load_list(k3, "l_k3")
+        gain = tile([P, 4], F32, "gain")
+        nc.sync.dma_start(gain[:], gs.rearrange("(p t) o -> p (t o)", t=4))
+        l_n3 = load_list(n3, "l_n3")
+        l_n4 = load_list(n4, "l_n4")
+        l_n5 = load_list(n5, "l_n5")
+        l_n6 = load_list(n6, "l_n6")
+        half = tile([P, 1], F32, "half")
+        nc.gpsimd.memset(half[:], 0.5)
+        b_scale = tile([P, 3 * H], U8, "b_scale")
+        nc.gpsimd.memset(b_scale[:].bitcast(I32), 0)
+        xh_s = tile([P, S], U8, "xh_s")
+        nc.gpsimd.memset(xh_s[:].bitcast(I32), 0)
+
+        def gather(dst, table, offsets):
+            nc.vector.tensor_copy(dst, table[:].indirect(offsets))
+
+        def halves(dst, table, offsets):
+            for u in range(2):
+                gather(dst[:, u * HALF : (u + 1) * HALF], table, offsets[:, 16 * u : 16 * (u + 1)])
+
+        def mm(acc, code, scale, rhs_w, rhs_s, start, stop):
+            nc.tensor.matmul_mx(out=acc, lhsT=code.bitcast(FP8X4), lhsT_scale=scale, rhs=rhs_w.bitcast(FP8X4), rhs_scale=rhs_s, start=start, stop=stop)
+
+        a_bytes = tile([P, 2 * H], U8, "a_bytes")
+        gather(a_bytes[:, 0:H], ds, l_k1[:])
+        gather(a_bytes[:, H : 2 * H], ds, l_k2[:])
+        xo_s = tile([P, S], U8, "xo_s")
+        gather(xo_s[:], xs, l_offs[:])
+        a_scale = tile([P, 4, 2 * P], U8, "a_scale")
+        nc.vector.tensor_copy(a_scale[:].rearrange("p t m -> p m t"), a_bytes[:].rearrange("p (m t) -> p m t", t=4))
+        flat = a_scale[:].rearrange("p t m -> p (t m)")
+        for r in range(1, 4):
+            nc.scalar.dma_start(flat[r:P:32, :].bitcast(I32), flat[8 * r : P : 32, :].bitcast(I32))
+        xt_s = tile([P, S], U8, "xt_s")
+        gather(xt_s[:], xs, l_two[:])
+        xo_w = tile([P, S], U32, "xo_w")
+        gather(xo_w[:], xw, l_offs[:])
+        xt_w = tile([P, S], U32, "xt_w")
+        gather(xt_w[:], xw, l_two[:])
+        a_words = [tile([P, H], U32, f"a_words{i}") for i in range(2)]
+        gather(a_words[0][:], dw, l_k1[:])
+        gather(a_words[1][:], dw, l_k2[:])
+        first = [tile([P, P], U32, f"first{i}") for i in range(2)]
+        rest = [tile([P, 3, P], U32, f"rest{i}") for i in range(2)]
+        for i in range(2):
+            nc.vector.tensor_copy(first[i][:], a_words[i][:, 0:H:4])
+        for i in range(2):
+            nc.vector.tensor_copy(rest[i][:].rearrange("p t m -> p m t"), a_words[i][:].rearrange("p (m t) -> p m t", t=4)[:, :, 1:4])
+
+        acc1 = [psum.tile([P, S], F32, name=f"acc1_{t}") for t in range(4)]
+        for t in range(4):
+            for i, (xwords, xscale) in enumerate(((xo_w, xo_s), (xt_w, xt_s))):
+                code = first[i][:] if t == 0 else rest[i][:, t - 1, :]
+                mm(acc1[t][:], code, a_scale[:, t, i * P : (i + 1) * P], xwords[:], xscale[:], i == 0, i == 1)
+
+        x2_w = tile([P, 2 * S], U32, "x2_w", "a_words0")
+        gather(x2_w[:, 0:S], xw, l_duo[:])
+        gather(x2_w[:, S:], xw, l_hz[:])
+        k4_w = [tile([P, HALF], U32, "k4_w0", "first1"), None]
+        gather(k4_w[0][:], dw, l_k4[:, 0:16])
+
+        h = [tile([P, S], F32, f"h{t}") for t in range(4)]
+        ub = [tile([P, S], F32, f"ub{t}") for t in range(4)]
+        z = tile([P, S, 4], BF16, "z")
+        pa = [tile([P, 2 * W], F32, f"pa{u}") for u in range(2)]
+        pb = [tile([P, 2 * W], F32, f"pb{u}") for u in range(2)]
+        size = [tile([P, 2 * W], F32, f"size{u}") for u in range(2)]
+        root = [tile([P, 2 * W], F32, f"root{u}") for u in range(2)]
+        big = [tile([P, 2 * W], F32, f"big{u}") for u in range(2)]
+        part = [tile([P, 2 * W], F32, f"part{u}") for u in range(2)]
+        ratio = [tile([P, 2 * W], F32, f"ratio{u}") for u in range(2)]
+
+        def cols(t):
+            return slice((t % 2) * W, (t % 2 + 1) * W)
+
+        def fetch(dst, t, offsets):
+            nc.scalar.activation(dst[t // 2][:, cols(t)], h[t][:].indirect(offsets[:]), ACT.Copy)
+
+        def put(src, t, offsets):
+            nc.scalar.activation(ub[t][:].indirect(offsets[:]), src[t // 2][:, cols(t)], ACT.Copy)
+
+        def weigh(t):
+            nc.vector.tensor_scalar(z[:, :, t], ub[t][:], gain[:, t : t + 1], None, ALU.mult)
+
+        nc.scalar.activation(h[0][:], acc1[0][:], ACT.Copy, scale=0.0625)
+        for t in range(1, 4):
+            nc.vector.tensor_scalar(h[t][:], acc1[t][:], 0.0625, None, ALU.mult)
+        for t in range(2):
+            fetch(pb, t, l_n2)
+            fetch(pa, t, l_n1)
+        xd_s = tile([P, S], U8, "xd_s", "h0")
+        gather(xd_s[:], xs, l_duo[:])
+        nc.scalar.activation(size[0][:], pb[0][:], ACT.Abs)
+        nc.vector.tensor_tensor(big[0][:], pa[0][:], pb[0][:], ALU.max)
+        b_bytes = tile([P, H + S], U8, "b_bytes", "h1")
+        halves(b_bytes, ds, l_k4)
+        gather(b_bytes[:, H:], xs, l_hz[:])
+        for r in range(4):
+            nc.sync.dma_start(b_scale[r:P:32, 0:H].bitcast(I32), b_bytes[8 * r : P : 32, 0:H].bitcast(I32))
+            nc.sync.dma_start(xh_s[r:P:32, :].bitcast(I32), b_bytes[16 * (r // 2) + r : P : 32, H:].bitcast(I32))
+        fetch(pb, 2, l_n2)
+        nc.scalar.activation(root[0][:], size[0][:], ACT.Abs_reciprocal_sqrt, bias=half[:])
+        fetch(pa, 2, l_n1)
+        fetch(pb, 3, l_n2)
+        fetch(pa, 3, l_n1)
+        nc.vector.tensor_tensor(part[0][:], pa[0][:], root[0][:], ALU.mult)
+        nc.vector.tensor_tensor(big[1][:], pa[1][:], pb[1][:], ALU.max)
+        nc.vector.tensor_tensor(ratio[0][:], part[0][:], root[0][:], ALU.mult)
+        c_bytes = tile([P, 2 * H], U8, "c_bytes", "h3")
+        halves(c_bytes[:, 0:H], ds, l_k5)
+        halves(c_bytes[:, H:], ds, l_k3)
+        for r in range(4):
+            nc.sync.dma_start(b_scale[r:P:32, H:].bitcast(I32), c_bytes[8 * r : P : 32, :].bitcast(I32))
+        nc.scalar.activation(size[1][:], pb[1][:], ACT.Abs)
+        put(big, 0, l_n2)
+        nc.scalar.activation(root[1][:], size[1][:], ACT.Abs_reciprocal_sqrt, bias=half[:])
+        put(big, 1, l_n2)
+        put(ratio, 0, l_n1)
+        put(ratio, 1, l_n1)
+        nc.vector.tensor_tensor(part[1][:], pa[1][:], root[1][:], ALU.mult)
+        k5_w = [tile([P, HALF], U32, "k5_w0", "size1"), None]
+        gather(k5_w[0][:], dw, l_k5[:, 0:16])
+        nc.vector.tensor_tensor(ratio[1][:], part[1][:], root[1][:], ALU.mult)
+        weigh(0)
+        k3_w = [tile([P, HALF], U32, "k3_w0", "ub0"), None]
+        weigh(1)
+        gather(k3_w[0][:], dw, l_k3[:, 0:16])
+        put(big, 2, l_n2)
+        put(big, 3, l_n2)
+        for t in range(2, 4):
+            put(ratio, t, l_n1)
+            weigh(t)
+        z_w = tile([P, S], U32, "z_w")
+        z_s = tile([P, S], U8, "z_s")
+        nc.vector.quantize_mx(out=z_w[:].bitcast(FP8X4), scales=z_s[:], in_=z[:].rearrange("p j t -> p (j t)"))
+
+        acc2 = [psum.tile([P, S], F32, name=f"acc2_{b}", tag=f"acc2_{b % 2}") for b in range(2)]
+        rhs = ((x2_w[:, 0:S], xd_s[:]), (x2_w[:, S:], xh_s[:]), (z_w[:], z_s[:]))
+
+        def product(i, b, code):
+            mm(acc2[b][:], code[:, cols(b)], b_scale[:, i * H + b * P : i * H + (b + 1) * P], rhs[i][0], rhs[i][1], i == 0, i == 2)
+
+        for i, code in enumerate((k4_w[0], k5_w[0], k3_w[0])):
+            for b in range(2):
+                product(i, b, code)
+
+        late = tile([P, 2 * HALF], U32, "late", "z")
+        gather(late[:, 0:HALF], dw, l_k4[:, 16:32])
+        gather(late[:, HALF:], dw, l_k5[:, 16:32])
+
+        h2 = [tile([P, S], F32, f"h2_{b}") for b in range(4)]
+        pa2 = [tile([P, W], F32, f"pa2_{b}") for b in range(4)]
+        pb2 = [tile([P, W], F32, f"pb2_{b}") for b in range(4)]
+        hi = [tile([P, W], F32, f"hi{b}") for b in range(4)]
+        lo = [tile([P, W], F32, f"lo{b}") for b in range(4)]
+        ub2 = [tile([P, S], F32, f"ub2_{b}") for b in range(4)]
+
+        def fetch2(b):
+            nc.scalar.activation(pa2[b][:], h2[b][:].indirect(l_n3[:]), ACT.Copy)
+            nc.scalar.activation(pb2[b][:], h2[b][:].indirect(l_n4[:]), ACT.Copy)
+            nc.vector.tensor_tensor(hi[b][:], pa2[b][:], pb2[b][:], ALU.max)
+            nc.vector.tensor_tensor(lo[b][:], pa2[b][:], pb2[b][:], ALU.min)
+
+        def put_hi(b):
+            nc.scalar.activation(ub2[b][:].indirect(l_n5[:]), hi[b][:], ACT.Copy)
+
+        def finish(b):
+            nc.scalar.activation(ub2[b][:].indirect(l_n6[:]), lo[b][:], ACT.Copy)
+            res = tile([P, S], F32, f"res{b}")
+            nc.vector.tensor_tensor(res[:], ub2[b][:], h2[b][:], ALU.subtract)
+            nc.sync.dma_start(out[b * P : (b + 1) * P, :], res[:])
+
+        nc.scalar.activation(h2[0][:], acc2[0][:], ACT.Copy, scale=0.0625)
+        nc.vector.tensor_scalar(h2[1][:], acc2[1][:], 0.0625, None, ALU.mult)
+        fetch2(0)
+        k3_late = tile([P, HALF], U32, "k3_late", "pa2_0")
+        gather(k3_late[:], dw, l_k3[:, 16:32])
+        fetch2(1)
+        acc2.extend(psum.tile([P, S], F32, name=f"acc2_{b}", tag=f"acc2_{b % 2}") for b in range(2, 4))
+        for i, code in enumerate((late[:, 0:HALF], late[:, HALF:], k3_late[:])):
+            for b in range(2, 4):
+                product(i, b, code)
+        for b in range(2, 4):
+            nc.vector.tensor_scalar(h2[b][:], acc2[b][:], 0.0625, None, ALU.mult)
+        put_hi(0)
+        put_hi(1)
+        for b in range(2):
+            finish(b)
+            fetch2(b + 2)
+        put_hi(2)
+        put_hi(3)
+        finish(2)
+        finish(3)

@@ -66,6 +66,8 @@ def tile_picked_mttzmthratiocpor_none_p_kernel(
         l_n6 = load_list(n6, "l_n6")
         half = tile([P, 1], F32, "half")
         nc.gpsimd.memset(half[:], 0.5)
+        warm = tile([P, 1], F32, "warm")
+        nc.scalar.activation(warm[:], half[:], ACT.Abs_reciprocal_sqrt, bias=half[:])
         b_scale = tile([P, 3 * H], U8, "b_scale")
         nc.gpsimd.memset(b_scale[:].bitcast(I32), 0)
         xh_s = tile([P, S], U8, "xh_s")

@@ -68,17 +68,28 @@ def tile_picked_mttzmthratiocpor_none_p_kernel(
         nc.gpsimd.memset(half[:], 0.5)
         warm = tile([P, 1], F32, "warm")
         nc.scalar.activation(warm[:], half[:], ACT.Abs_reciprocal_sqrt, bias=half[:])
-        b_scale = tile([P, 3 * H], U8, "b_scale")
-        nc.gpsimd.memset(b_scale[:].bitcast(I32), 0)
-        xh_s = tile([P, S], U8, "xh_s")
-        nc.gpsimd.memset(xh_s[:].bitcast(I32), 0)
+        b_scale = tile([P, 7, HALF], U8, "b_scale")
+        nc.gpsimd.memset(b_scale[:].rearrange("p a c -> p (a c)").bitcast(I32), 0)
 
         def gather(dst, table, offsets):
             nc.vector.tensor_copy(dst, table[:].indirect(offsets))
 
-        def halves(dst, table, offsets):
-            for u in range(2):
-                gather(dst[:, u * HALF : (u + 1) * HALF], table, offsets[:, 16 * u : 16 * (u + 1)])
+        def lower(offsets):
+            return offsets[:, 0:16]
+
+        def upper(offsets):
+            return offsets[:, 16:32]
+
+        def place(src, first, count):
+            dst = b_scale[:, first : first + count, :].rearrange("p a c -> p (a c)")
+            flat_src = src[:].rearrange("p a c -> p (a c)")
+            for r in range(4):
+                nc.sync.dma_start(dst[r:P:32, :].bitcast(I32), flat_src[9 * r : P : 32, :].bitcast(I32))
+
+        def picked(name, tag, table, offsets, dtype):
+            t = tile([P, S], dtype, name, tag)
+            gather(t[:], table, offsets)
+            return t
 
         def mm(acc, code, scale, rhs_w, rhs_s, start, stop):
             nc.tensor.matmul_mx(out=acc, lhsT=code.bitcast(FP8X4), lhsT_scale=scale, rhs=rhs_w.bitcast(FP8X4), rhs_scale=rhs_s, start=start, stop=stop)
@@ -115,11 +126,9 @@ def tile_picked_mttzmthratiocpor_none_p_kernel(
                 code = first[i][:] if t == 0 else rest[i][:, t - 1, :]
                 mm(acc1[t][:], code, a_scale[:, t, i * P : (i + 1) * P], xwords[:], xscale[:], i == 0, i == 1)
 
-        x2_w = tile([P, 2 * S], U32, "x2_w", "a_words0")
-        gather(x2_w[:, 0:S], xw, l_duo[:])
-        gather(x2_w[:, S:], xw, l_hz[:])
-        k4_w = [tile([P, HALF], U32, "k4_w0", "first1"), None]
-        gather(k4_w[0][:], dw, l_k4[:, 0:16])
+        xd_w = picked("xd_w", "a_words0", xw, l_duo[:], U32)
+        xh_w = picked("xh_w", "a_words1", xw, l_hz[:], U32)
+        k4_lo = picked("k4_lo", "first1", dw, lower(l_k4), U32)
 
         h = [tile([P, S], F32, f"h{t}") for t in range(4)]
         ub = [tile([P, S], F32, f"ub{t}") for t in range(4)]
@@ -135,8 +144,9 @@ def tile_picked_mttzmthratiocpor_none_p_kernel(
         def cols(t):
             return slice((t % 2) * W, (t % 2 + 1) * W)
 
-        def fetch(dst, t, offsets):
-            nc.scalar.activation(dst[t // 2][:, cols(t)], h[t][:].indirect(offsets[:]), ACT.Copy)
+        def fetch(t):
+            nc.scalar.activation(pb[t // 2][:, cols(t)], h[t][:].indirect(l_n2[:]), ACT.Copy)
+            nc.scalar.activation(pa[t // 2][:, cols(t)], h[t][:].indirect(l_n1[:]), ACT.Copy)
 
         def put(src, t, offsets):
             nc.scalar.activation(ub[t][:].indirect(offsets[:]), src[t // 2][:, cols(t)], ACT.Copy)
@@ -145,48 +155,38 @@ def tile_picked_mttzmthratiocpor_none_p_kernel(
             nc.vector.tensor_scalar(z[:, :, t], ub[t][:], gain[:, t : t + 1], None, ALU.mult)
 
         nc.scalar.activation(h[0][:], acc1[0][:], ACT.Copy, scale=0.0625)
-        for t in range(1, 4):
-            nc.vector.tensor_scalar(h[t][:], acc1[t][:], 0.0625, None, ALU.mult)
-        for t in range(2):
-            fetch(pb, t, l_n2)
-            fetch(pa, t, l_n1)
-        xd_s = tile([P, S], U8, "xd_s", "h0")
-        gather(xd_s[:], xs, l_duo[:])
-        nc.scalar.activation(size[0][:], pb[0][:], ACT.Abs)
+        fetch(0)
+        nc.scalar.activation(h[1][:], acc1[1][:], ACT.Copy, scale=0.0625)
+        nc.scalar.activation(size[0][:, cols(0)], pb[0][:, cols(0)], ACT.Abs)
+        nc.vector.tensor_scalar(h[2][:], acc1[2][:], 0.0625, None, ALU.mult)
+        xd_s = picked("xd_s", "h0", xs, l_duo[:], U8)
+        nc.vector.tensor_scalar(h[3][:], acc1[3][:], 0.0625, None, ALU.mult)
+        fetch(1)
+        nc.scalar.activation(size[0][:, cols(1)], pb[0][:, cols(1)], ACT.Abs)
         nc.vector.tensor_tensor(big[0][:], pa[0][:], pb[0][:], ALU.max)
-        b_bytes = tile([P, H + S], U8, "b_bytes", "h1")
-        halves(b_bytes, ds, l_k4)
-        gather(b_bytes[:, H:], xs, l_hz[:])
-        for r in range(4):
-            nc.sync.dma_start(b_scale[r:P:32, 0:H].bitcast(I32), b_bytes[8 * r : P : 32, 0:H].bitcast(I32))
-            nc.sync.dma_start(xh_s[r:P:32, :].bitcast(I32), b_bytes[16 * (r // 2) + r : P : 32, H:].bitcast(I32))
-        fetch(pb, 2, l_n2)
+        fetch(2)
         nc.scalar.activation(root[0][:], size[0][:], ACT.Abs_reciprocal_sqrt, bias=half[:])
-        fetch(pa, 2, l_n1)
-        fetch(pb, 3, l_n2)
-        fetch(pa, 3, l_n1)
+        fetch(3)
         nc.vector.tensor_tensor(part[0][:], pa[0][:], root[0][:], ALU.mult)
-        nc.vector.tensor_tensor(big[1][:], pa[1][:], pb[1][:], ALU.max)
+        nc.vector.scalar_tensor_tensor(size[1][:], pb[1][:], -1.0, pb[1][:], ALU.mult, ALU.max)
         nc.vector.tensor_tensor(ratio[0][:], part[0][:], root[0][:], ALU.mult)
-        c_bytes = tile([P, 2 * H], U8, "c_bytes", "h3")
-        halves(c_bytes[:, 0:H], ds, l_k5)
-        halves(c_bytes[:, H:], ds, l_k3)
-        for r in range(4):
-            nc.sync.dma_start(b_scale[r:P:32, H:].bitcast(I32), c_bytes[8 * r : P : 32, :].bitcast(I32))
-        nc.scalar.activation(size[1][:], pb[1][:], ACT.Abs)
+        nc.vector.tensor_tensor(big[1][:], pa[1][:], pb[1][:], ALU.max)
+        bytes1 = tile([P, 5, HALF], U8, "bytes1", "h3")
+        gather(bytes1[:, 0, :], xs, l_hz[:])
+        for i, offsets in enumerate((lower(l_k4), lower(l_k5), lower(l_k3), upper(l_k4))):
+            gather(bytes1[:, 1 + i, :], ds, offsets)
+        place(bytes1, 0, 5)
         put(big, 0, l_n2)
-        nc.scalar.activation(root[1][:], size[1][:], ACT.Abs_reciprocal_sqrt, bias=half[:])
         put(big, 1, l_n2)
+        nc.scalar.activation(root[1][:], size[1][:], ACT.Abs_reciprocal_sqrt, bias=half[:])
         put(ratio, 0, l_n1)
         put(ratio, 1, l_n1)
         nc.vector.tensor_tensor(part[1][:], pa[1][:], root[1][:], ALU.mult)
-        k5_w = [tile([P, HALF], U32, "k5_w0", "size1"), None]
-        gather(k5_w[0][:], dw, l_k5[:, 0:16])
+        k5_lo = picked("k5_lo", "size1", dw, lower(l_k5), U32)
         nc.vector.tensor_tensor(ratio[1][:], part[1][:], root[1][:], ALU.mult)
         weigh(0)
-        k3_w = [tile([P, HALF], U32, "k3_w0", "ub0"), None]
         weigh(1)
-        gather(k3_w[0][:], dw, l_k3[:, 0:16])
+        k3_lo = picked("k3_lo", "ub0", dw, lower(l_k3), U32)
         put(big, 2, l_n2)
         put(big, 3, l_n2)
         for t in range(2, 4):
@@ -196,19 +196,21 @@ def tile_picked_mttzmthratiocpor_none_p_kernel(
         z_s = tile([P, S], U8, "z_s")
         nc.vector.quantize_mx(out=z_w[:].bitcast(FP8X4), scales=z_s[:], in_=z[:].rearrange("p j t -> p (j t)"))
 
+        rhs = ((xd_w[:], xd_s[:]), (xh_w[:], b_scale[:, 0, :]), (z_w[:], z_s[:]))
         acc2 = [psum.tile([P, S], F32, name=f"acc2_{b}", tag=f"acc2_{b % 2}") for b in range(2)]
-        rhs = ((x2_w[:, 0:S], xd_s[:]), (x2_w[:, S:], xh_s[:]), (z_w[:], z_s[:]))
 
-        def product(i, b, code):
-            mm(acc2[b][:], code[:, cols(b)], b_scale[:, i * H + b * P : i * H + (b + 1) * P], rhs[i][0], rhs[i][1], i == 0, i == 2)
+        def product2(i, b, code, plane):
+            c = slice((b % 2) * P, (b % 2 + 1) * P)
+            mm(acc2[b][:], code[:, c], b_scale[:, plane, c], rhs[i][0], rhs[i][1], i == 0, i == 2)
 
-        for i, code in enumerate((k4_w[0], k5_w[0], k3_w[0])):
+        for i, code in enumerate((k4_lo, k5_lo, k3_lo)):
             for b in range(2):
-                product(i, b, code)
+                product2(i, b, code, 1 + i)
 
-        late = tile([P, 2 * HALF], U32, "late", "z")
-        gather(late[:, 0:HALF], dw, l_k4[:, 16:32])
-        gather(late[:, HALF:], dw, l_k5[:, 16:32])
+        bytes3 = tile([P, 2, HALF], U8, "bytes3", "z")
+        gather(bytes3[:, 0, :], ds, upper(l_k5))
+        gather(bytes3[:, 1, :], ds, upper(l_k3))
+        place(bytes3, 5, 2)
 
         h2 = [tile([P, S], F32, f"h2_{b}") for b in range(4)]
         pa2 = [tile([P, W], F32, f"pa2_{b}") for b in range(4)]
@@ -228,27 +230,28 @@ def tile_picked_mttzmthratiocpor_none_p_kernel(
 
         def finish(b):
             nc.scalar.activation(ub2[b][:].indirect(l_n6[:]), lo[b][:], ACT.Copy)
-            res = tile([P, S], F32, f"res{b}")
+            res = tile([P, S], F32, f"res{b}", ("pa2_1", "z_w", None, None)[b])
             nc.vector.tensor_tensor(res[:], ub2[b][:], h2[b][:], ALU.subtract)
             nc.sync.dma_start(out[b * P : (b + 1) * P, :], res[:])
 
         nc.scalar.activation(h2[0][:], acc2[0][:], ACT.Copy, scale=0.0625)
         nc.vector.tensor_scalar(h2[1][:], acc2[1][:], 0.0625, None, ALU.mult)
+        k4_hi = picked("k4_hi", "ub0", dw, upper(l_k4), U32)
         fetch2(0)
-        k3_late = tile([P, HALF], U32, "k3_late", "pa2_0")
-        gather(k3_late[:], dw, l_k3[:, 16:32])
+        k5_hi = picked("k5_hi", "pa2_0", dw, upper(l_k5), U32)
         fetch2(1)
+        k3_hi = picked("k3_hi", "pa2_1", dw, upper(l_k3), U32)
         acc2.extend(psum.tile([P, S], F32, name=f"acc2_{b}", tag=f"acc2_{b % 2}") for b in range(2, 4))
-        for i, code in enumerate((late[:, 0:HALF], late[:, HALF:], k3_late[:])):
-            for b in range(2, 4):
-                product(i, b, code)
         for b in range(2, 4):
+            for i, code in enumerate((k4_hi, k5_hi, k3_hi)):
+                product2(i, b, code, 4 + i)
             nc.vector.tensor_scalar(h2[b][:], acc2[b][:], 0.0625, None, ALU.mult)
         put_hi(0)
         put_hi(1)
-        for b in range(2):
-            finish(b)
-            fetch2(b + 2)
+        finish(0)
+        finish(1)
+        fetch2(2)
+        fetch2(3)
         put_hi(2)
         put_hi(3)
         finish(2)

from contextlib import ExitStack

import concourse.mybir as mybir

K, T, S, G, H, W = 512, 1024, 256, 2048, 512, 128
FLOPS = 5 * 2 * K * H * S

F32 = mybir.dt.float32
BF16 = mybir.dt.bfloat16
I32 = mybir.dt.int32
U32 = mybir.dt.uint32
U16 = mybir.dt.uint16
U8 = mybir.dt.uint8
FP8X4 = mybir.dt.float8_e4m3fn_x4
ALU = mybir.AluOpType
ACT = mybir.ActivationFunctionType
P = 128
HALF = H // 2


def tile_picked_mttzmthratiocpor_none_p_kernel(
    tc, x_words, x_scales, d_words, d_scales, gs, offs, k1, two, k2, n1, n2, k3, k4, duo, k5, hz, n3, n4, n5, n6, out
):
    nc = tc.nc
    with ExitStack() as ctx:
        lists = ctx.enter_context(tc.tile_pool(name="lists", bufs=1))
        sb = ctx.enter_context(tc.tile_pool(name="sb", bufs=1))
        psum = ctx.enter_context(tc.psum_pool(name="psum", bufs=1))

        def tile(shape, dtype, name, tag=None):
            return sb.tile(shape, dtype, name=name, tag=tag or name, align_bytes=64)

        def load_list(src, name):
            t = lists.tile(list(src.shape), U16, name=name)
            nc.sync.dma_start(t[:], src)
            return t

        ds = tile([P, G], U8, "ds")
        nc.sync.dma_start(ds[:].bitcast(I32), d_scales[0].bitcast(I32).unsqueeze(1).to_broadcast([16, 8, G // 4]))
        l_k1 = load_list(k1, "l_k1")
        l_k2 = load_list(k2, "l_k2")
        xs = tile([P, T], U8, "xs")
        for q in range(4):
            nc.sync.dma_start(
                xs[32 * q : 32 * (q + 1), :].bitcast(I32),
                x_scales[0][4 * q : 4 * (q + 1), :].bitcast(I32).unsqueeze(0).to_broadcast([8, 4, T // 4]),
            )
        xw = tile([P, T], U32, "xw")
        nc.sync.dma_start(xw[:].bitcast(I32), x_words[0].rearrange("p n t -> p (n t)").bitcast(I32))
        l_offs = load_list(offs, "l_offs")
        l_two = load_list(two, "l_two")
        dw = tile([P, G], U32, "dw")
        nc.sync.dma_start(dw[:].bitcast(I32), d_words[0].rearrange("p n t -> p (n t)").bitcast(I32))
        l_n2 = load_list(n2, "l_n2")
        l_n1 = load_list(n1, "l_n1")
        l_hz = load_list(hz, "l_hz")
        l_duo = load_list(duo, "l_duo")
        l_k4 = load_list(k4, "l_k4")
        l_k5 = load_list(k5, "l_k5")
        l_k3 = load_list(k3, "l_k3")
        gain = tile([P, 4], F32, "gain")
        nc.sync.dma_start(gain[:], gs.rearrange("(p t) o -> p (t o)", t=4))
        l_n3 = load_list(n3, "l_n3")
        l_n4 = load_list(n4, "l_n4")
        l_n5 = load_list(n5, "l_n5")
        l_n6 = load_list(n6, "l_n6")
        half = tile([P, 1], F32, "half")
        nc.gpsimd.memset(half[:], 0.5)
        warm = tile([P, 1], F32, "warm")
        nc.scalar.activation(warm[:], half[:], ACT.Abs_reciprocal_sqrt, bias=half[:])
        b_scale = tile([P, 7, HALF], U8, "b_scale")
        nc.gpsimd.memset(b_scale[:].rearrange("p a c -> p (a c)").bitcast(I32), 0)

        def gather(dst, table, offsets):
            nc.vector.tensor_copy(dst, table[:].indirect(offsets))

        def lower(offsets):
            return offsets[:, 0:16]

        def upper(offsets):
            return offsets[:, 16:32]

        def place(src, first, count):
            dst = b_scale[:, first : first + count, :].rearrange("p a c -> p (a c)")
            flat_src = src[:].rearrange("p a c -> p (a c)")
            for r in range(4):
                nc.sync.dma_start(dst[r:P:32, :].bitcast(I32), flat_src[9 * r : P : 32, :].bitcast(I32))

        def picked(name, tag, table, offsets, dtype):
            t = tile([P, S], dtype, name, tag)
            gather(t[:], table, offsets)
            return t

        def mm(acc, code, scale, rhs_w, rhs_s, start, stop):
            nc.tensor.matmul_mx(out=acc, lhsT=code.bitcast(FP8X4), lhsT_scale=scale, rhs=rhs_w.bitcast(FP8X4), rhs_scale=rhs_s, start=start, stop=stop)

        a_bytes = tile([P, 2 * H], U8, "a_bytes")
        gather(a_bytes[:, 0:H], ds, l_k1[:])
        gather(a_bytes[:, H : 2 * H], ds, l_k2[:])
        xo_s = tile([P, S], U8, "xo_s")
        gather(xo_s[:], xs, l_offs[:])
        a_scale = tile([P, 4, 2 * P], U8, "a_scale")
        nc.vector.tensor_copy(a_scale[:].rearrange("p t m -> p m t"), a_bytes[:].rearrange("p (m t) -> p m t", t=4))
        flat = a_scale[:].rearrange("p t m -> p (t m)")
        for r in range(1, 4):
            nc.scalar.dma_start(flat[r:P:32, :].bitcast(I32), flat[8 * r : P : 32, :].bitcast(I32))
        xt_s = tile([P, S], U8, "xt_s")
        gather(xt_s[:], xs, l_two[:])
        xo_w = tile([P, S], U32, "xo_w")
        gather(xo_w[:], xw, l_offs[:])
        xt_w = tile([P, S], U32, "xt_w")
        gather(xt_w[:], xw, l_two[:])
        a_words = [tile([P, H], U32, f"a_words{i}") for i in range(2)]
        gather(a_words[0][:], dw, l_k1[:])
        gather(a_words[1][:], dw, l_k2[:])
        first = [tile([P, P], U32, f"first{i}") for i in range(2)]
        rest = [tile([P, 3, P], U32, f"rest{i}") for i in range(2)]
        for i in range(2):
            nc.vector.tensor_copy(first[i][:], a_words[i][:, 0:H:4])
        for i in range(2):
            nc.vector.tensor_copy(rest[i][:].rearrange("p t m -> p m t"), a_words[i][:].rearrange("p (m t) -> p m t", t=4)[:, :, 1:4])

        acc1 = [psum.tile([P, S], F32, name=f"acc1_{t}") for t in range(4)]
        for t in range(4):
            for i, (xwords, xscale) in enumerate(((xo_w, xo_s), (xt_w, xt_s))):
                code = first[i][:] if t == 0 else rest[i][:, t - 1, :]
                mm(acc1[t][:], code, a_scale[:, t, i * P : (i + 1) * P], xwords[:], xscale[:], i == 0, i == 1)

        xd_w = picked("xd_w", "a_words0", xw, l_duo[:], U32)
        xh_w = picked("xh_w", "a_words1", xw, l_hz[:], U32)
        k4_lo = picked("k4_lo", "first1", dw, lower(l_k4), U32)

        h = [tile([P, S], F32, f"h{t}") for t in range(4)]
        ub = [tile([P, S], F32, f"ub{t}") for t in range(4)]
        z = tile([P, S, 4], BF16, "z")
        pa = [tile([P, 2 * W], F32, f"pa{u}") for u in range(2)]
        pb = [tile([P, 2 * W], F32, f"pb{u}") for u in range(2)]
        size = [tile([P, 2 * W], F32, f"size{u}") for u in range(2)]
        root = [tile([P, 2 * W], F32, f"root{u}") for u in range(2)]
        big = [tile([P, 2 * W], F32, f"big{u}") for u in range(2)]
        part = [tile([P, 2 * W], F32, f"part{u}") for u in range(2)]
        ratio = [tile([P, 2 * W], F32, f"ratio{u}") for u in range(2)]

        def cols(t):
            return slice((t % 2) * W, (t % 2 + 1) * W)

        def fetch(t):
            nc.scalar.activation(pb[t // 2][:, cols(t)], h[t][:].indirect(l_n2[:]), ACT.Copy)
            nc.scalar.activation(pa[t // 2][:, cols(t)], h[t][:].indirect(l_n1[:]), ACT.Copy)

        def put(src, t, offsets):
            nc.scalar.activation(ub[t][:].indirect(offsets[:]), src[t // 2][:, cols(t)], ACT.Copy)

        def weigh(t):
            nc.vector.tensor_scalar(z[:, :, t], ub[t][:], gain[:, t : t + 1], None, ALU.mult)

        nc.scalar.activation(h[0][:], acc1[0][:], ACT.Copy, scale=0.0625)
        fetch(0)
        nc.scalar.activation(h[1][:], acc1[1][:], ACT.Copy, scale=0.0625)
        nc.scalar.activation(size[0][:, cols(0)], pb[0][:, cols(0)], ACT.Abs)
        nc.vector.tensor_scalar(h[2][:], acc1[2][:], 0.0625, None, ALU.mult)
        xd_s = picked("xd_s", "h0", xs, l_duo[:], U8)
        nc.vector.tensor_scalar(h[3][:], acc1[3][:], 0.0625, None, ALU.mult)
        fetch(1)
        nc.scalar.activation(size[0][:, cols(1)], pb[0][:, cols(1)], ACT.Abs)
        nc.vector.tensor_tensor(big[0][:], pa[0][:], pb[0][:], ALU.max)
        fetch(2)
        nc.scalar.activation(root[0][:], size[0][:], ACT.Abs_reciprocal_sqrt, bias=half[:])
        fetch(3)
        nc.vector.tensor_tensor(part[0][:], pa[0][:], root[0][:], ALU.mult)
        nc.vector.scalar_tensor_tensor(size[1][:], pb[1][:], -1.0, pb[1][:], ALU.mult, ALU.max)
        nc.vector.tensor_tensor(ratio[0][:], part[0][:], root[0][:], ALU.mult)
        nc.vector.tensor_tensor(big[1][:], pa[1][:], pb[1][:], ALU.max)
        bytes1 = tile([P, 5, HALF], U8, "bytes1", "h3")
        gather(bytes1[:, 0, :], xs, l_hz[:])
        for i, offsets in enumerate((lower(l_k4), lower(l_k5), lower(l_k3), upper(l_k4))):
            gather(bytes1[:, 1 + i, :], ds, offsets)
        place(bytes1, 0, 5)
        put(big, 0, l_n2)
        put(big, 1, l_n2)
        nc.scalar.activation(root[1][:], size[1][:], ACT.Abs_reciprocal_sqrt, bias=half[:])
        put(ratio, 0, l_n1)
        put(ratio, 1, l_n1)
        nc.vector.tensor_tensor(part[1][:], pa[1][:], root[1][:], ALU.mult)
        k5_lo = picked("k5_lo", "size1", dw, lower(l_k5), U32)
        nc.vector.tensor_tensor(ratio[1][:], part[1][:], root[1][:], ALU.mult)
        weigh(0)
        weigh(1)
        k3_lo = picked("k3_lo", "ub0", dw, lower(l_k3), U32)
        put(big, 2, l_n2)
        put(big, 3, l_n2)
        for t in range(2, 4):
            put(ratio, t, l_n1)
            weigh(t)
        z_w = tile([P, S], U32, "z_w")
        z_s = tile([P, S], U8, "z_s")
        nc.vector.quantize_mx(out=z_w[:].bitcast(FP8X4), scales=z_s[:], in_=z[:].rearrange("p j t -> p (j t)"))

        rhs = ((xd_w[:], xd_s[:]), (xh_w[:], b_scale[:, 0, :]), (z_w[:], z_s[:]))
        acc2 = [psum.tile([P, S], F32, name=f"acc2_{b}", tag=f"acc2_{b % 2}") for b in range(2)]

        def product2(i, b, code, plane):
            c = slice((b % 2) * P, (b % 2 + 1) * P)
            mm(acc2[b][:], code[:, c], b_scale[:, plane, c], rhs[i][0], rhs[i][1], i == 0, i == 2)

        for i, code in enumerate((k4_lo, k5_lo, k3_lo)):
            for b in range(2):
                product2(i, b, code, 1 + i)

        bytes3 = tile([P, 2, HALF], U8, "bytes3", "z")
        gather(bytes3[:, 0, :], ds, upper(l_k5))
        gather(bytes3[:, 1, :], ds, upper(l_k3))
        place(bytes3, 5, 2)

        h2 = [tile([P, S], F32, f"h2_{b}") for b in range(4)]
        pa2 = [tile([P, W], F32, f"pa2_{b}") for b in range(4)]
        pb2 = [tile([P, W], F32, f"pb2_{b}") for b in range(4)]
        hi = [tile([P, W], F32, f"hi{b}") for b in range(4)]
        lo = [tile([P, W], F32, f"lo{b}") for b in range(4)]
        ub2 = [tile([P, S], F32, f"ub2_{b}") for b in range(4)]

        def fetch2(b):
            nc.scalar.activation(pa2[b][:], h2[b][:].indirect(l_n3[:]), ACT.Copy)
            nc.scalar.activation(pb2[b][:], h2[b][:].indirect(l_n4[:]), ACT.Copy)
            nc.vector.tensor_tensor(hi[b][:], pa2[b][:], pb2[b][:], ALU.max)
            nc.vector.tensor_tensor(lo[b][:], pa2[b][:], pb2[b][:], ALU.min)

        def put_hi(b):
            nc.scalar.activation(ub2[b][:].indirect(l_n5[:]), hi[b][:], ACT.Copy)

        def finish(b):
            nc.scalar.activation(ub2[b][:].indirect(l_n6[:]), lo[b][:], ACT.Copy)
            res = tile([P, S], F32, f"res{b}", ("pa2_1", "z_w", None, None)[b])
            nc.vector.tensor_tensor(res[:], ub2[b][:], h2[b][:], ALU.subtract)
            nc.sync.dma_start(out[b * P : (b + 1) * P, :], res[:])

        nc.scalar.activation(h2[0][:], acc2[0][:], ACT.Copy, scale=0.0625)
        nc.vector.tensor_scalar(h2[1][:], acc2[1][:], 0.0625, None, ALU.mult)
        k4_hi = picked("k4_hi", "ub0", dw, upper(l_k4), U32)
        fetch2(0)
        k5_hi = picked("k5_hi", "pa2_0", dw, upper(l_k5), U32)
        fetch2(1)
        k3_hi = picked("k3_hi", "pa2_1", dw, upper(l_k3), U32)
        acc2.extend(psum.tile([P, S], F32, name=f"acc2_{b}", tag=f"acc2_{b % 2}") for b in range(2, 4))
        for b in range(2, 4):
            for i, code in enumerate((k4_hi, k5_hi, k3_hi)):
                product2(i, b, code, 4 + i)
            nc.vector.tensor_scalar(h2[b][:], acc2[b][:], 0.0625, None, ALU.mult)
        put_hi(0)
        put_hi(1)
        finish(0)
        finish(1)
        fetch2(2)
        fetch2(3)
        put_hi(2)
        put_hi(3)
        finish(2)
        finish(3)
